import numpy as np
import ml_dtypes


def mxq(x, axis, fmt="e4m3"):
    dtype, down = {"e4m3": (ml_dtypes.float8_e4m3fn, 7), "e5m2": (ml_dtypes.float8_e5m2, 14)}[fmt]
    v = np.moveaxis(np.asarray(x, np.float32).astype(ml_dtypes.bfloat16).astype(np.float64), axis, -1)
    blocks = v.reshape(v.shape[:-1] + (-1, 32))
    amax = np.abs(blocks).max(-1, keepdims=True)
    byte = np.maximum(np.where(amax > 0, np.frexp(amax)[1] - 1 + 127, 0) - down, 1)
    scale = np.exp2(byte - 127.0)
    codes = (blocks / scale).astype(np.float32).astype(dtype).astype(np.float64)
    return np.moveaxis((codes * scale).reshape(v.shape), -1, axis)


WIDE = False


def mx_kscale(k, group=512):
    if not WIDE:
        return np.ones(k)
    levels = np.array([10, -10, 5, -5, 0])
    if group != 512:
        return np.exp2(np.random.permutation(np.resize(levels, k // group))).repeat(group)
    if k % 512:
        return np.exp2(np.random.permutation(np.resize(levels, k // 32))).repeat(32)
    a = np.empty((k // 512, 16))
    for p in range(k // 512):
        a[p, :8] = np.random.permutation(np.resize(levels, 8))
        for g in range(8):
            far = levels[np.abs(levels - a[p, g]) >= 10]
            a[p, g + 8] = far[np.random.randint(len(far))]
    return np.exp2(a.ravel()).repeat(32)


def f64(x):
    return np.asarray(x).astype(np.float64)


G, D, M, O, N = 2, 256, 256, 256, 512


def sgn(shape):
    return np.random.uniform(0.5, 2.0, shape) * np.where(np.random.standard_normal(shape) < 0, -1.0, 1.0)


def setup_inputs():
    n = np.random.standard_normal
    s_d = mx_kscale(D, 0)
    s_m = mx_kscale(M, 0)
    return {
        "x": (n((G, D, N)) * s_d[:, None]).astype(np.float32),
        "w1": (n((G, D, M)) / np.sqrt(D) / s_d[:, None]).astype(np.float32),
        "w2": (n((G, D, M)) / np.sqrt(D) / s_d[:, None]).astype(np.float32),
        "tp": (np.random.uniform(0.6, 2.0, (G, M, 1))).astype(np.float32),
        "hs": (sgn((G, M, 1)) * s_m[:, None]).astype(np.float32),
        "wo2": (n((G, M, O)) / np.sqrt(M) / s_m[:, None]).astype(np.float32),
        "ob": (0.5 * n((G, O, 1))).astype(np.float32),
        "osc": (np.random.uniform(0.5, 2.0, (G, O, 1))).astype(np.float32),
    }


def reference(x, w1, w2, tp, hs, wo2, ob, osc):
    w1q = mxq(f64(w1), 1, "e4m3")
    xq = mxq(f64(x), 1, "e4m3")
    z1 = w1q.transpose(0, 2, 1) @ xq
    w2q = mxq(f64(w2), 1, "e4m3")
    z2 = w2q.transpose(0, 2, 1) @ xq
    se = np.exp(z1 * f64(tp)) + np.exp(z2 * f64(tp))
    h = np.log(se) / f64(tp)
    hh = h * f64(hs)
    wo2q = mxq(f64(wo2), 1, "e4m3")
    hhq = mxq(hh, 1, "e4m3")
    y0 = wo2q.transpose(0, 2, 1) @ hhq
    y = np.tanh(y0 + f64(ob)) * f64(osc)
    return y

@@ -1,0 +1,191 @@
+from contextlib import ExitStack
+
+import concourse.mybir as mybir
+
+G, D, M, O, N = 2, 256, 256, 256, 512
+FLOPS = 2 * G * N * (2 * D * M + M * O)
+
+F32 = mybir.dt.float32
+BF16 = mybir.dt.bfloat16
+U32 = mybir.dt.uint32
+U8 = mybir.dt.uint8
+FP8X4 = mybir.dt.float8_e4m3fn_x4
+ACT = mybir.ActivationFunctionType
+ALU = mybir.AluOpType
+
+P = 128
+ROWS = 64
+PACK = 4
+T = 2
+NMM = 128
+HALF = N // 2
+CLAMP = 40.0
+BIG = 3.0e38
+X_SPLIT = 352
+
+
+def tile_rows_fsoftmaxoftwo_kernel(tc, x, w1, w2, tp, hs, wo2, ob, osc, out):
+    nc = tc.nc
+    with ExitStack() as ctx:
+        sb = ctx.enter_context(tc.tile_pool(name="sb", bufs=1))
+        ps = ctx.enter_context(tc.psum_pool(name="ps", bufs=1))
+        ctx.enter_context(tc.manual_schedule())
+
+        def new(name, shape, dtype):
+            return sb.tile(shape, dtype, name=name, align_bytes=64)
+
+        def load_rows(name, src, width):
+            raw = new(name, [P, PACK, width], F32)
+            nc.sync.dma_start(out=raw[:], in_=src.rearrange("g (p j) n -> (g p) j n", j=PACK))
+            return raw
+
+        def load_factor(name, src):
+            col = new(name, [P, G, T], F32)
+            nc.scalar.dma_start(out=col[:], in_=src.rearrange("g (q t) o -> q g (t o)", t=T))
+            return col[:].rearrange("q g t -> q (g t)")
+
+        def dealt(raw, t):
+            return raw[:].rearrange("p j (q t) -> p t q j", t=T)[:, t]
+
+        def quantize(name, grouped, width):
+            codes = new(name + "_codes", [P, width], U32)
+            scales = new(name + "_scales", [P, width], U8)
+            nc.vector.quantize_mx(out=codes[:].bitcast(FP8X4), scales=scales[:],
+                                  in_=grouped.rearrange("p n j -> p (n j)"))
+            return codes, scales
+
+        def product(bank, col0, g, stat, mov, mov_col0):
+            rows = slice(ROWS * g, ROWS * (g + 1))
+            cols = slice(mov_col0, mov_col0 + NMM)
+            nc.tensor.matmul_mx(out=bank[:, col0:col0 + NMM],
+                                lhsT=stat[0][rows, :].bitcast(FP8X4), lhsT_scale=stat[1][rows, :],
+                                rhs=mov[0][rows, cols].bitcast(FP8X4), rhs_scale=mov[1][rows, cols],
+                                start=True, stop=True)
+
+        tp_c = load_factor("tp_c", tp)
+        hs_c = load_factor("hs_c", hs)
+        ob_c = load_factor("ob_c", ob)
+        osc_c = load_factor("osc_c", osc)
+        x_raw = load_rows("x_raw", x, N)
+        w2_raw = load_rows("w2_raw", w2, M)
+        w1_raw = load_rows("w1_raw", w1, M)
+        wo_raw = load_rows("wo_raw", wo2, O)
+
+        small = [P, G * T]
+        inv_tp = new("inv_tp", small, F32)
+        hs_nz = new("hs_nz", small, F32)
+        gain = new("gain", small, F32)
+        inv_hs = new("inv_hs", small, F32)
+        open_hi = new("open_hi", small, F32)
+        open_lo = new("open_lo", small, F32)
+        rate = new("rate", small, F32)
+        hi = new("hi", small, F32)
+        lo = new("lo", small, F32)
+
+        x_lo = new("x_lo", [P, HALF, PACK], BF16)
+        x_hi = new("x_hi", [P, HALF, PACK], BF16)
+        x_t = x_raw[:].rearrange("p j n -> p n j")
+        nc.scalar.copy(out=x_hi[:, X_SPLIT - HALF:, :], in_=x_t[:, X_SPLIT:, :])
+        nc.vector.tensor_copy(out=x_lo[:], in_=x_t[:, :HALF, :])
+        nc.vector.tensor_copy(out=x_hi[:, :X_SPLIT - HALF, :], in_=x_t[:, HALF:X_SPLIT, :])
+
+        xq = [quantize("x_lo", x_lo[:], HALF), quantize("x_hi", x_hi[:], HALF)]
+        nc.vector.reciprocal(out=inv_tp[:], in_=tp_c)
+        nc.vector.scalar_tensor_tensor(out=hs_nz[:], in0=hs_c, scalar=0.0, in1=hs_c, op0=ALU.is_equal, op1=ALU.add)
+
+        w2g = [new("w2g%d" % t, [P, P, PACK], BF16) for t in range(T)]
+        w1g = [new("w1g%d" % t, [P, P, PACK], BF16) for t in range(T)]
+        wog = [new("wog%d" % t, [P, P, PACK], BF16) for t in range(T)]
+        nc.scalar.copy(out=w2g[1][:], in_=dealt(w2_raw, 1))
+        nc.vector.tensor_copy(out=w2g[0][:], in_=dealt(w2_raw, 0))
+        nc.vector.tensor_tensor(out=gain[:], in0=hs_c, in1=inv_tp[:], op=ALU.mult)
+        nc.vector.reciprocal(out=inv_hs[:], in_=hs_nz[:])
+        w2q1 = quantize("w2q1", w2g[1][:], P)
+        w2q = [quantize("w2q0", w2g[0][:], P), w2q1]
+        nc.vector.tensor_scalar(out=open_hi[:], in0=gain[:], scalar1=0.0, scalar2=BIG, op0=ALU.is_le, op1=ALU.mult)
+        nc.vector.tensor_scalar(out=open_lo[:], in0=gain[:], scalar1=0.0, scalar2=-BIG, op0=ALU.is_ge, op1=ALU.mult)
+        nc.scalar.copy(out=w1g[1][:], in_=dealt(w1_raw, 1))
+        nc.vector.tensor_copy(out=w1g[0][:], in_=dealt(w1_raw, 0))
+        nc.vector.tensor_tensor(out=rate[:], in0=tp_c, in1=inv_hs[:], op=ALU.mult)
+        nc.vector.scalar_tensor_tensor(out=hi[:], in0=gain[:], scalar=CLAMP, in1=open_hi[:], op0=ALU.mult, op1=ALU.add)
+        nc.vector.scalar_tensor_tensor(out=lo[:], in0=gain[:], scalar=CLAMP, in1=open_lo[:], op0=ALU.mult, op1=ALU.add)
+        w1q = [quantize("w1q%d" % t, w1g[t][:], P) for t in range(T)]
+
+        tiles = [(g, t) for t in range(T) for g in range(G)]
+        z1 = {gt: ps.tile([P, N], F32, name="z1_%d%d" % gt) for gt in tiles}
+        z2 = {gt: ps.tile([P, N], F32, name="z2_%d%d" % gt) for gt in tiles}
+        for banks, wq in ((z2, w2q), (z1, w1q)):
+            for t in range(T):
+                for c in range(N // NMM):
+                    for g in range(G):
+                        product(banks[(g, t)], c * NMM, g, wq[t], xq[c * NMM // HALF], c * NMM % HALF)
+
+        def col(tile, gt):
+            i = T * gt[0] + gt[1]
+            return tile[:, i:i + 1]
+
+        b = {gt: new("b%d%d" % gt, [P, N], F32) for gt in tiles}
+        d = {gt: new("d%d%d" % gt, [P, N], F32) for gt in tiles}
+        m = {gt: new("m%d%d" % gt, [P, N], F32) for gt in tiles}
+        q = {gt: new("q%d%d" % gt, [P, N], F32) for gt in tiles}
+        e = [new("e%d" % g, [P, T, N], F32) for g in range(G)]
+        for gt in tiles:
+            nc.scalar.activation(out=b[gt][:], in_=z2[gt][:], func=ACT.Copy, scale=col(hs_c, gt))
+
+        def diff(gt):
+            nc.vector.scalar_tensor_tensor(out=d[gt][:], in0=z1[gt][:], scalar=col(hs_c, gt), in1=b[gt][:],
+                                           op0=ALU.mult, op1=ALU.subtract)
+
+        def clamp(gt):
+            nc.vector.tensor_scalar(out=m[gt][:], in0=d[gt][:], scalar1=col(hi, gt), scalar2=col(lo, gt),
+                                    op0=ALU.min, op1=ALU.max)
+            nc.scalar.activation(out=e[gt[0]][:, gt[1], :], in_=m[gt][:], func=ACT.Exp, scale=col(rate, gt))
+
+        diff(tiles[0])
+        for i in range(1, len(tiles)):
+            diff(tiles[i])
+            clamp(tiles[i - 1])
+        clamp(tiles[-1])
+        for gt in tiles:
+            nc.vector.scalar_tensor_tensor(out=q[gt][:], in0=z1[gt][:], scalar=col(hs_c, gt), in1=m[gt][:],
+                                           op0=ALU.mult, op1=ALU.subtract)
+        for t in range(T):
+            nc.vector.tensor_copy(out=wog[t][:], in_=dealt(wo_raw, t))
+
+        moved = [new("moved%d" % h, [P, PACK, HALF], BF16) for h in range(2)]
+        for h in range(2):
+            cols = slice(h * HALF, (h + 1) * HALF)
+            for g in range(G):
+                lg = new("lg%d%d" % (h, g), [P, T, HALF], F32)
+                hh = new("hh%d%d" % (h, g), [P, T, HALF], BF16)
+                nc.scalar.activation(out=lg[:], in_=e[g][:, :, cols], func=ACT.Ln, bias=1.0)
+                for t in range(T):
+                    nc.vector.scalar_tensor_tensor(out=hh[:, t, :], in0=lg[:, t, :], scalar=col(gain, (g, t)),
+                                                   in1=q[(g, t)][:, cols], op0=ALU.mult, op1=ALU.add)
+                nc.sync.dma_start(
+                    out=moved[h][ROWS * g:ROWS * (g + 1)].rearrange("p (u t) n -> p u (t n)", t=T),
+                    in_=hh[:].rearrange("q t n -> q (t n)"))
+        woq = [quantize("woq%d" % t, wog[t][:], P) for t in range(T)]
+
+        th = {}
+        for h, banks in ((0, z2), (1, z1)):
+            hg = new("hg%d" % h, [P, HALF, PACK], BF16)
+            nc.vector.tensor_copy(out=hg[:], in_=moved[h][:].rearrange("p j n -> p n j"))
+            hq = quantize("hq%d" % h, hg[:], HALF)
+            for t in range(T):
+                for c in range(HALF // NMM):
+                    for g in range(G):
+                        product(banks[(g, t)], c * NMM, g, woq[t], hq, c * NMM)
+            for g in range(G):
+                for t in range(T):
+                    th[(h, g, t)] = new("th%d%d%d" % (h, g, t), [P, HALF], F32)
+                    nc.scalar.activation(out=th[(h, g, t)][:], in_=banks[(g, t)][:, :HALF], func=ACT.Tanh,
+                                         bias=col(ob_c, (g, t)))
+        for h in range(2):
+            cols = slice(h * HALF, (h + 1) * HALF)
+            for g in range(G):
+                y = new("y%d%d" % (h, g), [P, T, HALF], F32)
+                for t in range(T):
+                    nc.vector.tensor_scalar(out=y[:, t, :], in0=th[(h, g, t)][:], scalar1=col(osc_c, (g, t)),
+                                            scalar2=None, op0=ALU.mult)
+                nc.sync.dma_start(out=out[g].rearrange("(q t) n -> q t n", t=T)[:, :, cols], in_=y[:])

@@ -15,13 +15,14 @@ ALU = mybir.AluOpType
 
 P = 128
 ROWS = 64
+QUAD = 32
 PACK = 4
 T = 2
 NMM = 128
 HALF = N // 2
 CLAMP = 40.0
 BIG = 3.0e38
-X_SPLIT = 352
+X_SPLIT = 336
 
 
 def tile_rows_fsoftmaxoftwo_kernel(tc, x, w1, w2, tp, hs, wo2, ob, osc, out):
@@ -38,11 +39,6 @@ def tile_rows_fsoftmaxoftwo_kernel(tc, x, w1, w2, tp, hs, wo2, ob, osc, out):
             raw = new(name, [P, PACK, width], F32)
             nc.sync.dma_start(out=raw[:], in_=src.rearrange("g (p j) n -> (g p) j n", j=PACK))
             return raw
-
-        def load_factor(name, src):
-            col = new(name, [P, G, T], F32)
-            nc.scalar.dma_start(out=col[:], in_=src.rearrange("g (q t) o -> q g (t o)", t=T))
-            return col[:].rearrange("q g t -> q (g t)")
 
         def dealt(raw, t):
             return raw[:].rearrange("p j (q t) -> p t q j", t=T)[:, t]
@@ -62,14 +58,21 @@ def tile_rows_fsoftmaxoftwo_kernel(tc, x, w1, w2, tp, hs, wo2, ob, osc, out):
                                 rhs=mov[0][rows, cols].bitcast(FP8X4), rhs_scale=mov[1][rows, cols],
                                 start=True, stop=True)
 
-        tp_c = load_factor("tp_c", tp)
-        hs_c = load_factor("hs_c", hs)
-        ob_c = load_factor("ob_c", ob)
-        osc_c = load_factor("osc_c", osc)
+        fac_rows = new("fac_rows", [P, G, QUAD * T], F32)
+        nc.gpsimd.memset(fac_rows[:], 0.0)
+        for r, (src, queue) in enumerate(((hs, nc.sync), (tp, nc.sync), (ob, nc.scalar), (osc, nc.scalar))):
+            queue.dma_start(out=fac_rows[r:P:QUAD], in_=src.rearrange("g (s f) o -> s g (f o)", f=QUAD * T))
         x_raw = load_rows("x_raw", x, N)
         w2_raw = load_rows("w2_raw", w2, M)
         w1_raw = load_rows("w1_raw", w1, M)
         wo_raw = load_rows("wo_raw", wo2, O)
+
+        fac_dealt = new("fac_dealt", [P, G * T * QUAD], F32)
+        fac = new("fac", [P, G * T * QUAD], F32)
+        nc.vector.tensor_copy(out=fac_dealt[:].rearrange("p (g t a) -> p g t a", g=G, t=T),
+                              in_=fac_rows[:].rearrange("p g (a t) -> p g t a", t=T))
+        nc.vector.transpose(out=fac[:], in_=fac_dealt[:])
+        hs_c, tp_c, ob_c, osc_c = [fac[:, r::QUAD] for r in range(4)]
 
         small = [P, G * T]
         inv_tp = new("inv_tp", small, F32)
@@ -81,6 +84,10 @@ def tile_rows_fsoftmaxoftwo_kernel(tc, x, w1, w2, tp, hs, wo2, ob, osc, out):
         rate = new("rate", small, F32)
         hi = new("hi", small, F32)
         lo = new("lo", small, F32)
+        nc.vector.reciprocal(out=inv_tp[:], in_=tp_c)
+        nc.vector.scalar_tensor_tensor(out=hs_nz[:], in0=hs_c, scalar=0.0, in1=hs_c, op0=ALU.is_equal, op1=ALU.add)
+        nc.vector.tensor_tensor(out=gain[:], in0=hs_c, in1=inv_tp[:], op=ALU.mult)
+        nc.vector.reciprocal(out=inv_hs[:], in_=hs_nz[:])
 
         x_lo = new("x_lo", [P, HALF, PACK], BF16)
         x_hi = new("x_hi", [P, HALF, PACK], BF16)
@@ -90,20 +97,16 @@ def tile_rows_fsoftmaxoftwo_kernel(tc, x, w1, w2, tp, hs, wo2, ob, osc, out):
         nc.vector.tensor_copy(out=x_hi[:, :X_SPLIT - HALF, :], in_=x_t[:, HALF:X_SPLIT, :])
 
         xq = [quantize("x_lo", x_lo[:], HALF), quantize("x_hi", x_hi[:], HALF)]
-        nc.vector.reciprocal(out=inv_tp[:], in_=tp_c)
-        nc.vector.scalar_tensor_tensor(out=hs_nz[:], in0=hs_c, scalar=0.0, in1=hs_c, op0=ALU.is_equal, op1=ALU.add)
 
         w2g = [new("w2g%d" % t, [P, P, PACK], BF16) for t in range(T)]
         w1g = [new("w1g%d" % t, [P, P, PACK], BF16) for t in range(T)]
         wog = [new("wog%d" % t, [P, P, PACK], BF16) for t in range(T)]
         nc.scalar.copy(out=w2g[1][:], in_=dealt(w2_raw, 1))
         nc.vector.tensor_copy(out=w2g[0][:], in_=dealt(w2_raw, 0))
-        nc.vector.tensor_tensor(out=gain[:], in0=hs_c, in1=inv_tp[:], op=ALU.mult)
-        nc.vector.reciprocal(out=inv_hs[:], in_=hs_nz[:])
-        w2q1 = quantize("w2q1", w2g[1][:], P)
-        w2q = [quantize("w2q0", w2g[0][:], P), w2q1]
         nc.vector.tensor_scalar(out=open_hi[:], in0=gain[:], scalar1=0.0, scalar2=BIG, op0=ALU.is_le, op1=ALU.mult)
         nc.vector.tensor_scalar(out=open_lo[:], in0=gain[:], scalar1=0.0, scalar2=-BIG, op0=ALU.is_ge, op1=ALU.mult)
+        w2q1 = quantize("w2q1", w2g[1][:], P)
+        w2q = [quantize("w2q0", w2g[0][:], P), w2q1]
         nc.scalar.copy(out=w1g[1][:], in_=dealt(w1_raw, 1))
         nc.vector.tensor_copy(out=w1g[0][:], in_=dealt(w1_raw, 0))
         nc.vector.tensor_tensor(out=rate[:], in0=tp_c, in1=inv_hs[:], op=ALU.mult)
@@ -111,11 +114,15 @@ def tile_rows_fsoftmaxoftwo_kernel(tc, x, w1, w2, tp, hs, wo2, ob, osc, out):
         nc.vector.scalar_tensor_tensor(out=lo[:], in0=gain[:], scalar=CLAMP, in1=open_lo[:], op0=ALU.mult, op1=ALU.add)
         w1q = [quantize("w1q%d" % t, w1g[t][:], P) for t in range(T)]
 
+        for t in range(T):
+            nc.gpsimd.tensor_scalar(out=wog[t][:], in0=dealt(wo_raw, t), scalar1=1.0, scalar2=0.0,
+                                    op0=ALU.mult, op1=ALU.add)
+
         tiles = [(g, t) for t in range(T) for g in range(G)]
         z1 = {gt: ps.tile([P, N], F32, name="z1_%d%d" % gt) for gt in tiles}
         z2 = {gt: ps.tile([P, N], F32, name="z2_%d%d" % gt) for gt in tiles}
-        for banks, wq in ((z2, w2q), (z1, w1q)):
-            for t in range(T):
+        for t in range(T):
+            for banks, wq in ((z2, w2q), (z1, w1q)):
                 for c in range(N // NMM):
                     for g in range(G):
                         product(banks[(g, t)], c * NMM, g, wq[t], xq[c * NMM // HALF], c * NMM % HALF)
@@ -137,55 +144,62 @@ def tile_rows_fsoftmaxoftwo_kernel(tc, x, w1, w2, tp, hs, wo2, ob, osc, out):
                                            op0=ALU.mult, op1=ALU.subtract)
 
         def clamp(gt):
-            nc.vector.tensor_scalar(out=m[gt][:], in0=d[gt][:], scalar1=col(hi, gt), scalar2=col(lo, gt),
+            nc.gpsimd.tensor_scalar(out=m[gt][:], in0=d[gt][:], scalar1=col(hi, gt), scalar2=col(lo, gt),
                                     op0=ALU.min, op1=ALU.max)
             nc.scalar.activation(out=e[gt[0]][:, gt[1], :], in_=m[gt][:], func=ACT.Exp, scale=col(rate, gt))
 
-        diff(tiles[0])
-        for i in range(1, len(tiles)):
-            diff(tiles[i])
-            clamp(tiles[i - 1])
-        clamp(tiles[-1])
+        for gt in tiles:
+            diff(gt)
+            clamp(gt)
         for gt in tiles:
             nc.vector.scalar_tensor_tensor(out=q[gt][:], in0=z1[gt][:], scalar=col(hs_c, gt), in1=m[gt][:],
                                            op0=ALU.mult, op1=ALU.subtract)
-        for t in range(T):
-            nc.vector.tensor_copy(out=wog[t][:], in_=dealt(wo_raw, t))
+        woq = [quantize("woq%d" % t, wog[t][:], P) for t in range(T)]
 
-        moved = [new("moved%d" % h, [P, PACK, HALF], BF16) for h in range(2)]
-        for h in range(2):
-            cols = slice(h * HALF, (h + 1) * HALF)
+        chunks = range(N // NMM)
+        moved = [new("moved%d" % c, [P, PACK, NMM], BF16) for c in chunks]
+        for c in chunks:
+            cols = slice(c * NMM, (c + 1) * NMM)
             for g in range(G):
-                lg = new("lg%d%d" % (h, g), [P, T, HALF], F32)
-                hh = new("hh%d%d" % (h, g), [P, T, HALF], BF16)
+                lg = new("lg%d%d" % (c, g), [P, T, NMM], F32)
+                hh = new("hh%d%d" % (c, g), [P, T, NMM], BF16)
                 nc.scalar.activation(out=lg[:], in_=e[g][:, :, cols], func=ACT.Ln, bias=1.0)
                 for t in range(T):
                     nc.vector.scalar_tensor_tensor(out=hh[:, t, :], in0=lg[:, t, :], scalar=col(gain, (g, t)),
                                                    in1=q[(g, t)][:, cols], op0=ALU.mult, op1=ALU.add)
                 nc.sync.dma_start(
-                    out=moved[h][ROWS * g:ROWS * (g + 1)].rearrange("p (u t) n -> p u (t n)", t=T),
+                    out=moved[c][ROWS * g:ROWS * (g + 1)].rearrange("p (u t) n -> p u (t n)", t=T),
                     in_=hh[:].rearrange("q t n -> q (t n)"))
-        woq = [quantize("woq%d" % t, wog[t][:], P) for t in range(T)]
 
-        th = {}
-        for h, banks in ((0, z2), (1, z1)):
-            hg = new("hg%d" % h, [P, HALF, PACK], BF16)
-            nc.vector.tensor_copy(out=hg[:], in_=moved[h][:].rearrange("p j n -> p n j"))
-            hq = quantize("hq%d" % h, hg[:], HALF)
+        hg = [new("hg%d" % c, [P, NMM, PACK], BF16) for c in chunks]
+        th = {(h, g, t): new("th%d%d%d" % (h, g, t), [P, HALF], F32) for h in range(2) for g, t in tiles}
+
+        def interleave(c):
+            nc.vector.tensor_copy(out=hg[c][:], in_=moved[c][:].rearrange("p j n -> p n j"))
+
+        def second_layer(c):
+            hq = quantize("hq%d" % c, hg[c][:], NMM)
+            banks = (z2, z1)[c % 2]
+            col0 = c // 2 * NMM
             for t in range(T):
-                for c in range(HALF // NMM):
-                    for g in range(G):
-                        product(banks[(g, t)], c * NMM, g, woq[t], hq, c * NMM)
+                for g in range(G):
+                    product(banks[(g, t)], col0, g, woq[t], hq, 0)
             for g in range(G):
                 for t in range(T):
-                    th[(h, g, t)] = new("th%d%d%d" % (h, g, t), [P, HALF], F32)
-                    nc.scalar.activation(out=th[(h, g, t)][:], in_=banks[(g, t)][:, :HALF], func=ACT.Tanh,
+                    nc.scalar.activation(out=th[(c // 2, g, t)][:, c % 2 * NMM:(c % 2 + 1) * NMM], in_=banks[(g, t)][:, col0:col0 + NMM], func=ACT.Tanh,
                                          bias=col(ob_c, (g, t)))
-        for h in range(2):
-            cols = slice(h * HALF, (h + 1) * HALF)
+
+        interleave(0)
+        for c in chunks[1:]:
+            interleave(c)
+            second_layer(c - 1)
+        second_layer(chunks[-1])
+        for c0, c1 in ((0, HALF), (HALF, HALF + NMM), (HALF + NMM, N)):
+            cols = slice(c0, c1)
+            part = slice(c0 % HALF, c0 % HALF + c1 - c0)
             for g in range(G):
-                y = new("y%d%d" % (h, g), [P, T, HALF], F32)
+                y = new("y%d_%d" % (c0, g), [P, T, c1 - c0], F32)
                 for t in range(T):
-                    nc.vector.tensor_scalar(out=y[:, t, :], in0=th[(h, g, t)][:], scalar1=col(osc_c, (g, t)),
+                    nc.vector.tensor_scalar(out=y[:, t, :], in0=th[(c0 // HALF, g, t)][:, part], scalar1=col(osc_c, (g, t)),
                                             scalar2=None, op0=ALU.mult)
                 nc.sync.dma_start(out=out[g].rearrange("(q t) n -> q t n", t=T)[:, :, cols], in_=y[:])

@@ -23,6 +23,8 @@ HALF = N // 2
 CLAMP = 40.0
 BIG = 3.0e38
 X_SPLIT = 336
+WARM_PASSES = 16
+LAG = 2
 
 
 def tile_rows_fsoftmaxoftwo_kernel(tc, x, w1, w2, tp, hs, wo2, ob, osc, out):
@@ -60,12 +62,24 @@ def tile_rows_fsoftmaxoftwo_kernel(tc, x, w1, w2, tp, hs, wo2, ob, osc, out):
 
         fac_rows = new("fac_rows", [P, G, QUAD * T], F32)
         nc.gpsimd.memset(fac_rows[:], 0.0)
-        for r, (src, queue) in enumerate(((hs, nc.sync), (tp, nc.sync), (ob, nc.scalar), (osc, nc.scalar))):
-            queue.dma_start(out=fac_rows[r:P:QUAD], in_=src.rearrange("g (s f) o -> s g (f o)", f=QUAD * T))
-        x_raw = load_rows("x_raw", x, N)
         w2_raw = load_rows("w2_raw", w2, M)
+        for r, src in enumerate((hs, tp, ob, osc)):
+            nc.sync.dma_start(out=fac_rows[r:P:QUAD], in_=src.rearrange("g (s f) o -> s g (f o)", f=QUAD * T))
+        x_raw = load_rows("x_raw", x, N)
         w1_raw = load_rows("w1_raw", w1, M)
         wo_raw = load_rows("wo_raw", wo2, O)
+
+        w2g = [new("w2g%d" % t, [P, P, PACK], BF16) for t in range(T)]
+        w1g = [new("w1g%d" % t, [P, P, PACK], BF16) for t in range(T)]
+        wog = [new("wog%d" % t, [P, P, PACK], BF16) for t in range(T)]
+        nc.scalar.copy(out=w2g[1][:], in_=dealt(w2_raw, 1))
+        nc.vector.tensor_copy(out=w2g[0][:], in_=dealt(w2_raw, 0))
+        w2q = [quantize("w2q%d" % t, w2g[t][:], P) for t in range(T)]
+
+        warm = ps.tile([P, NMM], F32, name="warm")
+        for i in range(WARM_PASSES):
+            nc.tensor.matmul_mx(out=warm[:], lhsT=w2q[0][0][:].bitcast(FP8X4), lhsT_scale=w2q[0][1][:],
+                                rhs=w2q[0][0][:].bitcast(FP8X4), rhs_scale=w2q[0][1][:], start=True, stop=True)
 
         fac_dealt = new("fac_dealt", [P, G * T * QUAD], F32)
         fac = new("fac", [P, G * T * QUAD], F32)
@@ -88,6 +102,11 @@ def tile_rows_fsoftmaxoftwo_kernel(tc, x, w1, w2, tp, hs, wo2, ob, osc, out):
         nc.vector.scalar_tensor_tensor(out=hs_nz[:], in0=hs_c, scalar=0.0, in1=hs_c, op0=ALU.is_equal, op1=ALU.add)
         nc.vector.tensor_tensor(out=gain[:], in0=hs_c, in1=inv_tp[:], op=ALU.mult)
         nc.vector.reciprocal(out=inv_hs[:], in_=hs_nz[:])
+        nc.vector.tensor_scalar(out=open_hi[:], in0=gain[:], scalar1=0.0, scalar2=BIG, op0=ALU.is_le, op1=ALU.mult)
+        nc.vector.tensor_scalar(out=open_lo[:], in0=gain[:], scalar1=0.0, scalar2=-BIG, op0=ALU.is_ge, op1=ALU.mult)
+        nc.vector.tensor_tensor(out=rate[:], in0=tp_c, in1=inv_hs[:], op=ALU.mult)
+        nc.vector.scalar_tensor_tensor(out=hi[:], in0=gain[:], scalar=CLAMP, in1=open_hi[:], op0=ALU.mult, op1=ALU.add)
+        nc.vector.scalar_tensor_tensor(out=lo[:], in0=gain[:], scalar=CLAMP, in1=open_lo[:], op0=ALU.mult, op1=ALU.add)
 
         x_lo = new("x_lo", [P, HALF, PACK], BF16)
         x_hi = new("x_hi", [P, HALF, PACK], BF16)
@@ -98,20 +117,8 @@ def tile_rows_fsoftmaxoftwo_kernel(tc, x, w1, w2, tp, hs, wo2, ob, osc, out):
 
         xq = [quantize("x_lo", x_lo[:], HALF), quantize("x_hi", x_hi[:], HALF)]
 
-        w2g = [new("w2g%d" % t, [P, P, PACK], BF16) for t in range(T)]
-        w1g = [new("w1g%d" % t, [P, P, PACK], BF16) for t in range(T)]
-        wog = [new("wog%d" % t, [P, P, PACK], BF16) for t in range(T)]
-        nc.scalar.copy(out=w2g[1][:], in_=dealt(w2_raw, 1))
-        nc.vector.tensor_copy(out=w2g[0][:], in_=dealt(w2_raw, 0))
-        nc.vector.tensor_scalar(out=open_hi[:], in0=gain[:], scalar1=0.0, scalar2=BIG, op0=ALU.is_le, op1=ALU.mult)
-        nc.vector.tensor_scalar(out=open_lo[:], in0=gain[:], scalar1=0.0, scalar2=-BIG, op0=ALU.is_ge, op1=ALU.mult)
-        w2q1 = quantize("w2q1", w2g[1][:], P)
-        w2q = [quantize("w2q0", w2g[0][:], P), w2q1]
         nc.scalar.copy(out=w1g[1][:], in_=dealt(w1_raw, 1))
         nc.vector.tensor_copy(out=w1g[0][:], in_=dealt(w1_raw, 0))
-        nc.vector.tensor_tensor(out=rate[:], in0=tp_c, in1=inv_hs[:], op=ALU.mult)
-        nc.vector.scalar_tensor_tensor(out=hi[:], in0=gain[:], scalar=CLAMP, in1=open_hi[:], op0=ALU.mult, op1=ALU.add)
-        nc.vector.scalar_tensor_tensor(out=lo[:], in0=gain[:], scalar=CLAMP, in1=open_lo[:], op0=ALU.mult, op1=ALU.add)
         w1q = [quantize("w1q%d" % t, w1g[t][:], P) for t in range(T)]
 
         for t in range(T):
@@ -120,12 +127,13 @@ def tile_rows_fsoftmaxoftwo_kernel(tc, x, w1, w2, tp, hs, wo2, ob, osc, out):
 
         tiles = [(g, t) for t in range(T) for g in range(G)]
         z1 = {gt: ps.tile([P, N], F32, name="z1_%d%d" % gt) for gt in tiles}
-        z2 = {gt: ps.tile([P, N], F32, name="z2_%d%d" % gt) for gt in tiles}
-        for t in range(T):
-            for banks, wq in ((z2, w2q), (z1, w1q)):
-                for c in range(N // NMM):
-                    for g in range(G):
-                        product(banks[(g, t)], c * NMM, g, wq[t], xq[c * NMM // HALF], c * NMM % HALF)
+        z2 = {gt: ps.tile([P, N], F32, name="z2_%d%d" % gt) for gt in tiles if gt != (0, 1)}
+        z2[(0, 1)] = z2[(0, 0)]
+
+        def first_layer(banks, wq):
+            for c in range(N // NMM):
+                for g in range(G):
+                    product(banks[g], c * NMM, g, wq, xq[c * NMM // HALF], c * NMM % HALF)
 
         def col(tile, gt):
             i = T * gt[0] + gt[1]
@@ -136,20 +144,28 @@ def tile_rows_fsoftmaxoftwo_kernel(tc, x, w1, w2, tp, hs, wo2, ob, osc, out):
         m = {gt: new("m%d%d" % gt, [P, N], F32) for gt in tiles}
         q = {gt: new("q%d%d" % gt, [P, N], F32) for gt in tiles}
         e = [new("e%d" % g, [P, T, N], F32) for g in range(G)]
-        for gt in tiles:
-            nc.scalar.activation(out=b[gt][:], in_=z2[gt][:], func=ACT.Copy, scale=col(hs_c, gt))
+        for t in range(T):
+            first_layer([z2[(g, t)] for g in range(G)], w2q[t])
+            first_layer([z1[(g, t)] for g in range(G)], w1q[t])
+            for g in range(G):
+                nc.scalar.activation(out=b[(g, t)][:], in_=z2[(g, t)][:], func=ACT.Copy, scale=col(hs_c, (g, t)))
 
         def diff(gt):
             nc.vector.scalar_tensor_tensor(out=d[gt][:], in0=z1[gt][:], scalar=col(hs_c, gt), in1=b[gt][:],
                                            op0=ALU.mult, op1=ALU.subtract)
 
         def clamp(gt):
-            nc.gpsimd.tensor_scalar(out=m[gt][:], in0=d[gt][:], scalar1=col(hi, gt), scalar2=col(lo, gt),
-                                    op0=ALU.min, op1=ALU.max)
+            engine = nc.vector if gt[1] else nc.gpsimd
+            engine.tensor_scalar(out=m[gt][:], in0=d[gt][:], scalar1=col(hi, gt), scalar2=col(lo, gt),
+                                 op0=ALU.min, op1=ALU.max)
             nc.scalar.activation(out=e[gt[0]][:, gt[1], :], in_=m[gt][:], func=ACT.Exp, scale=col(rate, gt))
 
-        for gt in tiles:
+        for gt in tiles[:G]:
             diff(gt)
+            clamp(gt)
+        for gt in tiles[G:]:
+            diff(gt)
+        for gt in tiles[G:]:
             clamp(gt)
         for gt in tiles:
             nc.vector.scalar_tensor_tensor(out=q[gt][:], in0=z1[gt][:], scalar=col(hs_c, gt), in1=m[gt][:],
@@ -171,35 +187,30 @@ def tile_rows_fsoftmaxoftwo_kernel(tc, x, w1, w2, tp, hs, wo2, ob, osc, out):
                     out=moved[c][ROWS * g:ROWS * (g + 1)].rearrange("p (u t) n -> p u (t n)", t=T),
                     in_=hh[:].rearrange("q t n -> q (t n)"))
 
-        hg = [new("hg%d" % c, [P, NMM, PACK], BF16) for c in chunks]
-        th = {(h, g, t): new("th%d%d%d" % (h, g, t), [P, HALF], F32) for h in range(2) for g, t in tiles}
+        th = {}
 
-        def interleave(c):
-            nc.vector.tensor_copy(out=hg[c][:], in_=moved[c][:].rearrange("p j n -> p n j"))
+        def finish(c, t):
+            y = new("y%d%d" % (c, t), [P, G, NMM], F32)
+            for g in range(G):
+                nc.vector.tensor_scalar(out=y[:, g, :], in0=th[(c, g, t)][:], scalar1=col(osc_c, (g, t)),
+                                        scalar2=None, op0=ALU.mult)
+            nc.sync.dma_start(out=out.rearrange("g (q t) n -> t q g n", t=T)[t][:, :, c * NMM:(c + 1) * NMM], in_=y[:])
 
-        def second_layer(c):
-            hq = quantize("hq%d" % c, hg[c][:], NMM)
-            banks = (z2, z1)[c % 2]
-            col0 = c // 2 * NMM
+        for c in chunks:
+            hg = new("hg%d" % c, [P, NMM, PACK], BF16)
+            nc.vector.tensor_copy(out=hg[:], in_=moved[c][:].rearrange("p j n -> p n j"))
+            if c >= LAG:
+                finish(c - LAG, 0)
+            hq = quantize("hq%d" % c, hg[:], NMM)
+            if c >= LAG:
+                finish(c - LAG, 1)
+            banks = {(g, t): (z2[(g, 0)], z1[(g, 0)], z1[(g, 1)])[(T * c + t) % 3] for g, t in tiles}
+            for g, t in tiles:
+                product(banks[(g, t)], 0, g, woq[t], hq, 0)
+            for g, t in tiles:
+                th[(c, g, t)] = new("th%d%d%d" % (c, g, t), [P, NMM], F32)
+                nc.scalar.activation(out=th[(c, g, t)][:], in_=banks[(g, t)][:, :NMM], func=ACT.Tanh,
+                                     bias=col(ob_c, (g, t)))
+        for c in chunks[-LAG:]:
             for t in range(T):
-                for g in range(G):
-                    product(banks[(g, t)], col0, g, woq[t], hq, 0)
-            for g in range(G):
-                for t in range(T):
-                    nc.scalar.activation(out=th[(c // 2, g, t)][:, c % 2 * NMM:(c % 2 + 1) * NMM], in_=banks[(g, t)][:, col0:col0 + NMM], func=ACT.Tanh,
-                                         bias=col(ob_c, (g, t)))
-
-        interleave(0)
-        for c in chunks[1:]:
-            interleave(c)
-            second_layer(c - 1)
-        second_layer(chunks[-1])
-        for c0, c1 in ((0, HALF), (HALF, HALF + NMM), (HALF + NMM, N)):
-            cols = slice(c0, c1)
-            part = slice(c0 % HALF, c0 % HALF + c1 - c0)
-            for g in range(G):
-                y = new("y%d_%d" % (c0, g), [P, T, c1 - c0], F32)
-                for t in range(T):
-                    nc.vector.tensor_scalar(out=y[:, t, :], in0=th[(c0 // HALF, g, t)][:, part], scalar1=col(osc_c, (g, t)),
-                                            scalar2=None, op0=ALU.mult)
-                nc.sync.dma_start(out=out[g].rearrange("(q t) n -> q t n", t=T)[:, :, cols], in_=y[:])
+                finish(c, t)

@@ -22,9 +22,9 @@ NMM = 128
 HALF = N // 2
 CLAMP = 40.0
 BIG = 3.0e38
-X_SPLIT = 336
-WARM_PASSES = 16
+X_SPLIT = 168
 LAG = 2
+RUN = 4
 
 
 def tile_rows_fsoftmaxoftwo_kernel(tc, x, w1, w2, tp, hs, wo2, ob, osc, out):
@@ -43,7 +43,13 @@ def tile_rows_fsoftmaxoftwo_kernel(tc, x, w1, w2, tp, hs, wo2, ob, osc, out):
             return raw
 
         def dealt(raw, t):
-            return raw[:].rearrange("p j (q t) -> p t q j", t=T)[:, t]
+            return raw[:].rearrange("p j (c i t) -> p t c j i", t=T, i=2)[:, t]
+
+        def words(grouped, run):
+            return grouped.rearrange("p (c i) j -> p c j i", i=run)
+
+        def runs(rows):
+            return rows.rearrange("p j (c i) -> p c j i", i=RUN)
 
         def quantize(name, grouped, width):
             codes = new(name + "_codes", [P, width], U32)
@@ -62,24 +68,12 @@ def tile_rows_fsoftmaxoftwo_kernel(tc, x, w1, w2, tp, hs, wo2, ob, osc, out):
 
         fac_rows = new("fac_rows", [P, G, QUAD * T], F32)
         nc.gpsimd.memset(fac_rows[:], 0.0)
+        for r, (src, queue) in enumerate(((hs, nc.sync), (tp, nc.sync), (ob, nc.scalar), (osc, nc.scalar))):
+            queue.dma_start(out=fac_rows[r:P:QUAD], in_=src.rearrange("g (s f) o -> s g (f o)", f=QUAD * T))
         w2_raw = load_rows("w2_raw", w2, M)
-        for r, src in enumerate((hs, tp, ob, osc)):
-            nc.sync.dma_start(out=fac_rows[r:P:QUAD], in_=src.rearrange("g (s f) o -> s g (f o)", f=QUAD * T))
-        x_raw = load_rows("x_raw", x, N)
+        x_raw = [load_rows("x_raw%d" % h, x[:, :, h * HALF:(h + 1) * HALF], HALF) for h in range(2)]
         w1_raw = load_rows("w1_raw", w1, M)
         wo_raw = load_rows("wo_raw", wo2, O)
-
-        w2g = [new("w2g%d" % t, [P, P, PACK], BF16) for t in range(T)]
-        w1g = [new("w1g%d" % t, [P, P, PACK], BF16) for t in range(T)]
-        wog = [new("wog%d" % t, [P, P, PACK], BF16) for t in range(T)]
-        nc.scalar.copy(out=w2g[1][:], in_=dealt(w2_raw, 1))
-        nc.vector.tensor_copy(out=w2g[0][:], in_=dealt(w2_raw, 0))
-        w2q = [quantize("w2q%d" % t, w2g[t][:], P) for t in range(T)]
-
-        warm = ps.tile([P, NMM], F32, name="warm")
-        for i in range(WARM_PASSES):
-            nc.tensor.matmul_mx(out=warm[:], lhsT=w2q[0][0][:].bitcast(FP8X4), lhsT_scale=w2q[0][1][:],
-                                rhs=w2q[0][0][:].bitcast(FP8X4), rhs_scale=w2q[0][1][:], start=True, stop=True)
 
         fac_dealt = new("fac_dealt", [P, G * T * QUAD], F32)
         fac = new("fac", [P, G * T * QUAD], F32)
@@ -98,42 +92,46 @@ def tile_rows_fsoftmaxoftwo_kernel(tc, x, w1, w2, tp, hs, wo2, ob, osc, out):
         rate = new("rate", small, F32)
         hi = new("hi", small, F32)
         lo = new("lo", small, F32)
+
         nc.vector.reciprocal(out=inv_tp[:], in_=tp_c)
         nc.vector.scalar_tensor_tensor(out=hs_nz[:], in0=hs_c, scalar=0.0, in1=hs_c, op0=ALU.is_equal, op1=ALU.add)
+
+        w2g = [new("w2g%d" % t, [P, P, PACK], BF16) for t in range(T)]
+        w1g = [new("w1g%d" % t, [P, P, PACK], BF16) for t in range(T)]
+        wog = [new("wog%d" % t, [P, P, PACK], BF16) for t in range(T)]
+        nc.scalar.copy(out=words(w2g[1][:], 2), in_=dealt(w2_raw, 1))
+        nc.vector.tensor_copy(out=words(w2g[0][:], 2), in_=dealt(w2_raw, 0))
         nc.vector.tensor_tensor(out=gain[:], in0=hs_c, in1=inv_tp[:], op=ALU.mult)
         nc.vector.reciprocal(out=inv_hs[:], in_=hs_nz[:])
+        w2q = [quantize("w2q%d" % t, w2g[t][:], P) for t in range(T)]
+
         nc.vector.tensor_scalar(out=open_hi[:], in0=gain[:], scalar1=0.0, scalar2=BIG, op0=ALU.is_le, op1=ALU.mult)
         nc.vector.tensor_scalar(out=open_lo[:], in0=gain[:], scalar1=0.0, scalar2=-BIG, op0=ALU.is_ge, op1=ALU.mult)
         nc.vector.tensor_tensor(out=rate[:], in0=tp_c, in1=inv_hs[:], op=ALU.mult)
+
+        def cast_x(h):
+            grouped = new("xg%d" % h, [P, HALF, PACK], BF16)
+            nc.scalar.copy(out=words(grouped[:, X_SPLIT:, :], RUN), in_=runs(x_raw[h][:, :, X_SPLIT:]))
+            nc.vector.tensor_copy(out=words(grouped[:, :X_SPLIT, :], RUN), in_=runs(x_raw[h][:, :, :X_SPLIT]))
+            return grouped
+
+        xg = cast_x(0)
         nc.vector.scalar_tensor_tensor(out=hi[:], in0=gain[:], scalar=CLAMP, in1=open_hi[:], op0=ALU.mult, op1=ALU.add)
         nc.vector.scalar_tensor_tensor(out=lo[:], in0=gain[:], scalar=CLAMP, in1=open_lo[:], op0=ALU.mult, op1=ALU.add)
+        xq = [quantize("xq0", xg[:], HALF)]
+        xq.append(quantize("xq1", cast_x(1)[:], HALF))
 
-        x_lo = new("x_lo", [P, HALF, PACK], BF16)
-        x_hi = new("x_hi", [P, HALF, PACK], BF16)
-        x_t = x_raw[:].rearrange("p j n -> p n j")
-        nc.scalar.copy(out=x_hi[:, X_SPLIT - HALF:, :], in_=x_t[:, X_SPLIT:, :])
-        nc.vector.tensor_copy(out=x_lo[:], in_=x_t[:, :HALF, :])
-        nc.vector.tensor_copy(out=x_hi[:, :X_SPLIT - HALF, :], in_=x_t[:, HALF:X_SPLIT, :])
-
-        xq = [quantize("x_lo", x_lo[:], HALF), quantize("x_hi", x_hi[:], HALF)]
-
-        nc.scalar.copy(out=w1g[1][:], in_=dealt(w1_raw, 1))
-        nc.vector.tensor_copy(out=w1g[0][:], in_=dealt(w1_raw, 0))
+        nc.scalar.copy(out=words(w1g[1][:], 2), in_=dealt(w1_raw, 1))
+        nc.vector.tensor_copy(out=words(w1g[0][:], 2), in_=dealt(w1_raw, 0))
         w1q = [quantize("w1q%d" % t, w1g[t][:], P) for t in range(T)]
-
-        for t in range(T):
-            nc.gpsimd.tensor_scalar(out=wog[t][:], in0=dealt(wo_raw, t), scalar1=1.0, scalar2=0.0,
-                                    op0=ALU.mult, op1=ALU.add)
+        nc.vector.tensor_copy(out=words(wog[0][:], 2), in_=dealt(wo_raw, 0))
 
         tiles = [(g, t) for t in range(T) for g in range(G)]
         z1 = {gt: ps.tile([P, N], F32, name="z1_%d%d" % gt) for gt in tiles}
-        z2 = {gt: ps.tile([P, N], F32, name="z2_%d%d" % gt) for gt in tiles if gt != (0, 1)}
-        z2[(0, 1)] = z2[(0, 0)]
+        z2 = {gt: ps.tile([P, N], F32, name="z2_%d%d" % gt) for gt in tiles}
 
-        def first_layer(banks, wq):
-            for c in range(N // NMM):
-                for g in range(G):
-                    product(banks[g], c * NMM, g, wq, xq[c * NMM // HALF], c * NMM % HALF)
+        def first_layer(banks, wq, t, g, c):
+            product(banks[(g, t)], c * NMM, g, wq[t], xq[c * NMM // HALF], c * NMM % HALF)
 
         def col(tile, gt):
             i = T * gt[0] + gt[1]
@@ -144,33 +142,42 @@ def tile_rows_fsoftmaxoftwo_kernel(tc, x, w1, w2, tp, hs, wo2, ob, osc, out):
         m = {gt: new("m%d%d" % gt, [P, N], F32) for gt in tiles}
         q = {gt: new("q%d%d" % gt, [P, N], F32) for gt in tiles}
         e = [new("e%d" % g, [P, T, N], F32) for g in range(G)]
-        for t in range(T):
-            first_layer([z2[(g, t)] for g in range(G)], w2q[t])
-            first_layer([z1[(g, t)] for g in range(G)], w1q[t])
+        def second_branch(t, h):
+            for c in range(h * HALF // NMM, (h + 1) * HALF // NMM):
+                for g in range(G):
+                    first_layer(z2, w2q, t, g, c)
+
+        def first_branch(t):
             for g in range(G):
-                nc.scalar.activation(out=b[(g, t)][:], in_=z2[(g, t)][:], func=ACT.Copy, scale=col(hs_c, (g, t)))
+                for c in range(N // NMM):
+                    first_layer(z1, w1q, t, g, c)
+
+        second_branch(0, 0)
+        second_branch(1, 0)
+        for t in range(T):
+            second_branch(t, 1)
+            first_branch(t)
+        for gt in tiles:
+            nc.scalar.activation(out=b[gt][:], in_=z2[gt][:], func=ACT.Copy, scale=col(hs_c, gt))
 
         def diff(gt):
             nc.vector.scalar_tensor_tensor(out=d[gt][:], in0=z1[gt][:], scalar=col(hs_c, gt), in1=b[gt][:],
                                            op0=ALU.mult, op1=ALU.subtract)
 
         def clamp(gt):
-            engine = nc.vector if gt[1] else nc.gpsimd
-            engine.tensor_scalar(out=m[gt][:], in0=d[gt][:], scalar1=col(hi, gt), scalar2=col(lo, gt),
-                                 op0=ALU.min, op1=ALU.max)
+            nc.vector.tensor_scalar(out=m[gt][:], in0=d[gt][:], scalar1=col(hi, gt), scalar2=col(lo, gt),
+                                    op0=ALU.min, op1=ALU.max)
             nc.scalar.activation(out=e[gt[0]][:, gt[1], :], in_=m[gt][:], func=ACT.Exp, scale=col(rate, gt))
 
-        for gt in tiles[:G]:
-            diff(gt)
-            clamp(gt)
-        for gt in tiles[G:]:
-            diff(gt)
-        for gt in tiles[G:]:
-            clamp(gt)
+        for t in range(T):
+            for g in range(G):
+                diff((g, t))
+            for g in range(G):
+                clamp((g, t))
         for gt in tiles:
             nc.vector.scalar_tensor_tensor(out=q[gt][:], in0=z1[gt][:], scalar=col(hs_c, gt), in1=m[gt][:],
                                            op0=ALU.mult, op1=ALU.subtract)
-        woq = [quantize("woq%d" % t, wog[t][:], P) for t in range(T)]
+        nc.vector.tensor_copy(out=words(wog[1][:], 2), in_=dealt(wo_raw, 1))
 
         chunks = range(N // NMM)
         moved = [new("moved%d" % c, [P, PACK, NMM], BF16) for c in chunks]
@@ -187,6 +194,7 @@ def tile_rows_fsoftmaxoftwo_kernel(tc, x, w1, w2, tp, hs, wo2, ob, osc, out):
                     out=moved[c][ROWS * g:ROWS * (g + 1)].rearrange("p (u t) n -> p u (t n)", t=T),
                     in_=hh[:].rearrange("q t n -> q (t n)"))
 
+        woq = [quantize("woq%d" % t, wog[t][:], P) for t in range(T)]
         th = {}
 
         def finish(c, t):
@@ -198,13 +206,13 @@ def tile_rows_fsoftmaxoftwo_kernel(tc, x, w1, w2, tp, hs, wo2, ob, osc, out):
 
         for c in chunks:
             hg = new("hg%d" % c, [P, NMM, PACK], BF16)
-            nc.vector.tensor_copy(out=hg[:], in_=moved[c][:].rearrange("p j n -> p n j"))
+            nc.vector.tensor_copy(out=words(hg[:], RUN), in_=runs(moved[c][:]))
             if c >= LAG:
                 finish(c - LAG, 0)
             hq = quantize("hq%d" % c, hg[:], NMM)
             if c >= LAG:
                 finish(c - LAG, 1)
-            banks = {(g, t): (z2[(g, 0)], z1[(g, 0)], z1[(g, 1)])[(T * c + t) % 3] for g, t in tiles}
+            banks = (z2, z1)[c % 2]
             for g, t in tiles:
                 product(banks[(g, t)], 0, g, woq[t], hq, 0)
             for g, t in tiles:

from contextlib import ExitStack

import concourse.mybir as mybir

G, D, M, O, N = 2, 256, 256, 256, 512
FLOPS = 2 * G * N * (2 * D * M + M * O)

F32 = mybir.dt.float32
BF16 = mybir.dt.bfloat16
U32 = mybir.dt.uint32
U8 = mybir.dt.uint8
FP8X4 = mybir.dt.float8_e4m3fn_x4
ACT = mybir.ActivationFunctionType
ALU = mybir.AluOpType

P = 128
ROWS = 64
QUAD = 32
PACK = 4
T = 2
NMM = 128
HALF = N // 2
CLAMP = 40.0
BIG = 3.0e38
X_SPLIT = 168
LAG = 2
RUN = 4


def tile_rows_fsoftmaxoftwo_kernel(tc, x, w1, w2, tp, hs, wo2, ob, osc, out):
    nc = tc.nc
    with ExitStack() as ctx:
        sb = ctx.enter_context(tc.tile_pool(name="sb", bufs=1))
        ps = ctx.enter_context(tc.psum_pool(name="ps", bufs=1))
        ctx.enter_context(tc.manual_schedule())

        def new(name, shape, dtype):
            return sb.tile(shape, dtype, name=name, align_bytes=64)

        def load_rows(name, src, width):
            raw = new(name, [P, PACK, width], F32)
            nc.sync.dma_start(out=raw[:], in_=src.rearrange("g (p j) n -> (g p) j n", j=PACK))
            return raw

        def dealt(raw, t):
            return raw[:].rearrange("p j (c i t) -> p t c j i", t=T, i=2)[:, t]

        def words(grouped, run):
            return grouped.rearrange("p (c i) j -> p c j i", i=run)

        def runs(rows):
            return rows.rearrange("p j (c i) -> p c j i", i=RUN)

        def quantize(name, grouped, width):
            codes = new(name + "_codes", [P, width], U32)
            scales = new(name + "_scales", [P, width], U8)
            nc.vector.quantize_mx(out=codes[:].bitcast(FP8X4), scales=scales[:],
                                  in_=grouped.rearrange("p n j -> p (n j)"))
            return codes, scales

        def product(bank, col0, g, stat, mov, mov_col0):
            rows = slice(ROWS * g, ROWS * (g + 1))
            cols = slice(mov_col0, mov_col0 + NMM)
            nc.tensor.matmul_mx(out=bank[:, col0:col0 + NMM],
                                lhsT=stat[0][rows, :].bitcast(FP8X4), lhsT_scale=stat[1][rows, :],
                                rhs=mov[0][rows, cols].bitcast(FP8X4), rhs_scale=mov[1][rows, cols],
                                start=True, stop=True)

        fac_rows = new("fac_rows", [P, G, QUAD * T], F32)
        nc.gpsimd.memset(fac_rows[:], 0.0)
        for r, (src, queue) in enumerate(((hs, nc.sync), (tp, nc.sync), (ob, nc.scalar), (osc, nc.scalar))):
            queue.dma_start(out=fac_rows[r:P:QUAD], in_=src.rearrange("g (s f) o -> s g (f o)", f=QUAD * T))
        w2_raw = load_rows("w2_raw", w2, M)
        x_raw = [load_rows("x_raw%d" % h, x[:, :, h * HALF:(h + 1) * HALF], HALF) for h in range(2)]
        w1_raw = load_rows("w1_raw", w1, M)
        wo_raw = load_rows("wo_raw", wo2, O)

        fac_dealt = new("fac_dealt", [P, G * T * QUAD], F32)
        fac = new("fac", [P, G * T * QUAD], F32)
        nc.vector.tensor_copy(out=fac_dealt[:].rearrange("p (g t a) -> p g t a", g=G, t=T),
                              in_=fac_rows[:].rearrange("p g (a t) -> p g t a", t=T))
        nc.vector.transpose(out=fac[:], in_=fac_dealt[:])
        hs_c, tp_c, ob_c, osc_c = [fac[:, r::QUAD] for r in range(4)]

        small = [P, G * T]
        inv_tp = new("inv_tp", small, F32)
        hs_nz = new("hs_nz", small, F32)
        gain = new("gain", small, F32)
        inv_hs = new("inv_hs", small, F32)
        open_hi = new("open_hi", small, F32)
        open_lo = new("open_lo", small, F32)
        rate = new("rate", small, F32)
        hi = new("hi", small, F32)
        lo = new("lo", small, F32)

        nc.vector.reciprocal(out=inv_tp[:], in_=tp_c)
        nc.vector.scalar_tensor_tensor(out=hs_nz[:], in0=hs_c, scalar=0.0, in1=hs_c, op0=ALU.is_equal, op1=ALU.add)

        w2g = [new("w2g%d" % t, [P, P, PACK], BF16) for t in range(T)]
        w1g = [new("w1g%d" % t, [P, P, PACK], BF16) for t in range(T)]
        wog = [new("wog%d" % t, [P, P, PACK], BF16) for t in range(T)]
        nc.scalar.copy(out=words(w2g[1][:], 2), in_=dealt(w2_raw, 1))
        nc.vector.tensor_copy(out=words(w2g[0][:], 2), in_=dealt(w2_raw, 0))
        nc.vector.tensor_tensor(out=gain[:], in0=hs_c, in1=inv_tp[:], op=ALU.mult)
        nc.vector.reciprocal(out=inv_hs[:], in_=hs_nz[:])
        w2q = [quantize("w2q%d" % t, w2g[t][:], P) for t in range(T)]

        nc.vector.tensor_scalar(out=open_hi[:], in0=gain[:], scalar1=0.0, scalar2=BIG, op0=ALU.is_le, op1=ALU.mult)
        nc.vector.tensor_scalar(out=open_lo[:], in0=gain[:], scalar1=0.0, scalar2=-BIG, op0=ALU.is_ge, op1=ALU.mult)
        nc.vector.tensor_tensor(out=rate[:], in0=tp_c, in1=inv_hs[:], op=ALU.mult)

        def cast_x(h):
            grouped = new("xg%d" % h, [P, HALF, PACK], BF16)
            nc.scalar.copy(out=words(grouped[:, X_SPLIT:, :], RUN), in_=runs(x_raw[h][:, :, X_SPLIT:]))
            nc.vector.tensor_copy(out=words(grouped[:, :X_SPLIT, :], RUN), in_=runs(x_raw[h][:, :, :X_SPLIT]))
            return grouped

        xg = cast_x(0)
        nc.vector.scalar_tensor_tensor(out=hi[:], in0=gain[:], scalar=CLAMP, in1=open_hi[:], op0=ALU.mult, op1=ALU.add)
        nc.vector.scalar_tensor_tensor(out=lo[:], in0=gain[:], scalar=CLAMP, in1=open_lo[:], op0=ALU.mult, op1=ALU.add)
        xq = [quantize("xq0", xg[:], HALF)]
        xq.append(quantize("xq1", cast_x(1)[:], HALF))

        nc.scalar.copy(out=words(w1g[1][:], 2), in_=dealt(w1_raw, 1))
        nc.vector.tensor_copy(out=words(w1g[0][:], 2), in_=dealt(w1_raw, 0))
        w1q = [quantize("w1q%d" % t, w1g[t][:], P) for t in range(T)]
        nc.vector.tensor_copy(out=words(wog[0][:], 2), in_=dealt(wo_raw, 0))

        tiles = [(g, t) for t in range(T) for g in range(G)]
        z1 = {gt: ps.tile([P, N], F32, name="z1_%d%d" % gt) for gt in tiles}
        z2 = {gt: ps.tile([P, N], F32, name="z2_%d%d" % gt) for gt in tiles}

        def first_layer(banks, wq, t, g, c):
            product(banks[(g, t)], c * NMM, g, wq[t], xq[c * NMM // HALF], c * NMM % HALF)

        def col(tile, gt):
            i = T * gt[0] + gt[1]
            return tile[:, i:i + 1]

        b = {gt: new("b%d%d" % gt, [P, N], F32) for gt in tiles}
        d = {gt: new("d%d%d" % gt, [P, N], F32) for gt in tiles}
        m = {gt: new("m%d%d" % gt, [P, N], F32) for gt in tiles}
        q = {gt: new("q%d%d" % gt, [P, N], F32) for gt in tiles}
        e = [new("e%d" % g, [P, T, N], F32) for g in range(G)]
        def second_branch(t, h):
            for c in range(h * HALF // NMM, (h + 1) * HALF // NMM):
                for g in range(G):
                    first_layer(z2, w2q, t, g, c)

        def first_branch(t):
            for g in range(G):
                for c in range(N // NMM):
                    first_layer(z1, w1q, t, g, c)

        second_branch(0, 0)
        second_branch(1, 0)
        for t in range(T):
            second_branch(t, 1)
            first_branch(t)
        for gt in tiles:
            nc.scalar.activation(out=b[gt][:], in_=z2[gt][:], func=ACT.Copy, scale=col(hs_c, gt))

        def diff(gt):
            nc.vector.scalar_tensor_tensor(out=d[gt][:], in0=z1[gt][:], scalar=col(hs_c, gt), in1=b[gt][:],
                                           op0=ALU.mult, op1=ALU.subtract)

        def clamp(gt):
            nc.vector.tensor_scalar(out=m[gt][:], in0=d[gt][:], scalar1=col(hi, gt), scalar2=col(lo, gt),
                                    op0=ALU.min, op1=ALU.max)
            nc.scalar.activation(out=e[gt[0]][:, gt[1], :], in_=m[gt][:], func=ACT.Exp, scale=col(rate, gt))

        for t in range(T):
            for g in range(G):
                diff((g, t))
            for g in range(G):
                clamp((g, t))
        for gt in tiles:
            nc.vector.scalar_tensor_tensor(out=q[gt][:], in0=z1[gt][:], scalar=col(hs_c, gt), in1=m[gt][:],
                                           op0=ALU.mult, op1=ALU.subtract)
        nc.vector.tensor_copy(out=words(wog[1][:], 2), in_=dealt(wo_raw, 1))

        chunks = range(N // NMM)
        moved = [new("moved%d" % c, [P, PACK, NMM], BF16) for c in chunks]
        for c in chunks:
            cols = slice(c * NMM, (c + 1) * NMM)
            for g in range(G):
                lg = new("lg%d%d" % (c, g), [P, T, NMM], F32)
                hh = new("hh%d%d" % (c, g), [P, T, NMM], BF16)
                nc.scalar.activation(out=lg[:], in_=e[g][:, :, cols], func=ACT.Ln, bias=1.0)
                for t in range(T):
                    nc.vector.scalar_tensor_tensor(out=hh[:, t, :], in0=lg[:, t, :], scalar=col(gain, (g, t)),
                                                   in1=q[(g, t)][:, cols], op0=ALU.mult, op1=ALU.add)
                nc.sync.dma_start(
                    out=moved[c][ROWS * g:ROWS * (g + 1)].rearrange("p (u t) n -> p u (t n)", t=T),
                    in_=hh[:].rearrange("q t n -> q (t n)"))

        woq = [quantize("woq%d" % t, wog[t][:], P) for t in range(T)]
        th = {}

        def finish(c, t):
            y = new("y%d%d" % (c, t), [P, G, NMM], F32)
            for g in range(G):
                nc.vector.tensor_scalar(out=y[:, g, :], in0=th[(c, g, t)][:], scalar1=col(osc_c, (g, t)),
                                        scalar2=None, op0=ALU.mult)
            nc.sync.dma_start(out=out.rearrange("g (q t) n -> t q g n", t=T)[t][:, :, c * NMM:(c + 1) * NMM], in_=y[:])

        for c in chunks:
            hg = new("hg%d" % c, [P, NMM, PACK], BF16)
            nc.vector.tensor_copy(out=words(hg[:], RUN), in_=runs(moved[c][:]))
            if c >= LAG:
                finish(c - LAG, 0)
            hq = quantize("hq%d" % c, hg[:], NMM)
            if c >= LAG:
                finish(c - LAG, 1)
            banks = (z2, z1)[c % 2]
            for g, t in tiles:
                product(banks[(g, t)], 0, g, woq[t], hq, 0)
            for g, t in tiles:
                th[(c, g, t)] = new("th%d%d%d" % (c, g, t), [P, NMM], F32)
                nc.scalar.activation(out=th[(c, g, t)][:], in_=banks[(g, t)][:, :NMM], func=ACT.Tanh,
                                     bias=col(ob_c, (g, t)))
        for c in chunks[-LAG:]:
            for t in range(T):
                finish(c, t)
